import numpy as np
CORES = [3,7,11,15,131,135,139,143]
N = 8
TK = 512
D = 128 * N
EPS = 0.01
def setup_inputs(rng):
    x = rng.standard_normal((N, 128, TK), dtype=np.float32) * (0.5 + np.abs(rng.standard_normal((1, 1, TK), dtype=np.float32))) + rng.standard_normal((1, 1, TK), dtype=np.float32)
    return {"x": x, "dy": rng.standard_normal((N, 128, TK), dtype=np.float32) + 0.5 * x + rng.standard_normal((1, 1, TK), dtype=np.float32)}
def reference(x, dy):
    X, DY = x.astype(np.float64), dy.astype(np.float64)
    mu = X.sum(axis=(0, 1)) / D
    rs = 1.0 / np.sqrt(((X - mu) ** 2).sum(axis=(0, 1)) / D + EPS)
    n = (X - mu) * rs
    a = DY.sum(axis=(0, 1)) / D; c = (DY * n).sum(axis=(0, 1)) / D
    return {"dx": (rs * (DY - a - n * c)).astype(np.float32)}

@@ -1,0 +1,196 @@
+from concourse.bass import DstId, RemoteDMATransfer
+from concourse.mybir import AluOpType, AxisListType, ActivationFunctionType
+
+N = 8
+TK = 512
+D = 128 * N
+EPS = 0.01
+NBLK = 4
+NPH = 1
+NB = NBLK // NPH
+W = 4 * NB
+
+SCRATCH = {
+    "xs": ("sbuf", [128, TK], "float32"),
+    "dys": ("sbuf", [128, TK], "float32"),
+    "ones": ("sbuf", [128, 128], "float32"),
+    "ident": ("sbuf", [128, 128], "float32"),
+    "xT": ("sbuf", [128, TK], "float32"),
+    "jq": ("sbuf", [128, TK], "float32"),
+    "prod": ("sbuf", [128, TK], "float32"),
+    "jp": ("sbuf", [128, TK], "float32"),
+    "land": ("sbuf", [128, N * 16], "float32"),
+    "cf": ("sbuf", [128, 16 * 16], "float32"),
+    "cs": ("sbuf", [128, 16], "float32"),
+    "u": ("sbuf", [128, TK], "float32"),
+    "inn": ("sbuf", [128, TK], "float32"),
+    "diag": ("sbuf", [128, TK], "float32"),
+    "outb": ("sbuf", [128, TK], "float32"),
+}
+for _j in range(NBLK):
+    SCRATCH["px%d" % _j] = ("psum", [128, 512], "float32")
+    SCRATCH["pd%d" % _j] = ("psum", [128, 512], "float32")
+
+SEMAPHORES = ["c_ones", "c_id", "vc", "sc", "sent"]
+for _h in range(2):
+    SEMAPHORES += ["ldx%d" % _h, "ldd%d" % _h, "ev%d" % _h, "st%d" % _h]
+for _j in range(NBLK):
+    SEMAPHORES += [_s + str(_j) for _s in ("tx", "td", "ex", "pm", "iv", "dg", "bk")]
+for _p in range(NPH):
+    SEMAPHORES += [_s + str(_p) for _s in ("ss", "vs", "arr", "vv", "vq")]
+
+
+def rank_program(g, core, T, topo):
+    rank = T.rank_of(core)
+    if rank is None:
+        return
+    sem = T.sem
+    A, ACT = AluOpType, ActivationFunctionType
+    te, ve, sa, sy = g.tensor, g.vector, g.scalar, g.sync
+
+    def blk(j):
+        return slice(128 * j, 128 * j + 128)
+
+    def col(j, s):
+        p, jj = divmod(j, NB)
+        return p * N * W + rank * W + s * NB + jj
+
+    px = [T["px%d" % j] for j in range(NBLK)]
+    pd = [T["pd%d" % j] for j in range(NBLK)]
+
+    for h in range(2):
+        c = slice(256 * h, 256 * h + 256)
+        sy.dma_start(T.xs[:, c], T.x[:, c]).then_inc(sem["ldx%d" % h], 16)
+        sy.dma_start(T.dys[:, c], T.dy[:, c]).then_inc(sem["ldd%d" % h], 16)
+
+    ve.memset(T.ones[:], 1.0).then_inc(sem.c_ones, 1)
+    g.wait_ge(sem.c_ones, 1)
+    g.affine_select(T.ident[:], T.ones[:], [[-1, 128]], A.is_equal, 0.0, 0, 1).then_inc(sem.c_id, 1)
+
+    te.wait_ge(sem.c_id, 1)
+    for h in range(2):
+        js = (2 * h, 2 * h + 1)
+        te.wait_ge(sem["ldx%d" % h], 16)
+        for j in js:
+            te.transpose(px[j][:, 0:128], T.xs[:, blk(j)], T.ident[:]).then_inc(sem["tx%d" % j], 1)
+        te.wait_ge(sem["ldd%d" % h], 16)
+        for j in js:
+            te.transpose(pd[j][:, 0:128], T.dys[:, blk(j)], T.ident[:]).then_inc(sem["td%d" % j], 1)
+        for j in js:
+            p = j // NB
+            sa.wait_ge(sem["tx%d" % j], 1)
+            sa.activation(T.xT[:, blk(j)], px[j][:, 0:128], ACT.Copy,
+                          accum_out=T.land[:, col(j, 0):col(j, 0) + 1]).then_inc(sem["ex%d" % j], 1)
+            sa.activation(T.jq[:, blk(j)], px[j][:, 0:128], ACT.Square,
+                          accum_out=T.land[:, col(j, 2):col(j, 2) + 1]).then_inc(sem["ss%d" % p], 1)
+        for j in js:
+            p = j // NB
+            ve.wait_ge(sem["td%d" % j], 1)
+            ve.wait_ge(sem["ex%d" % j], 1)
+            ve.tensor_tensor(T.prod[:, blk(j)], T.xT[:, blk(j)], pd[j][:, 0:128], A.mult).then_inc(sem["pm%d" % j], 1)
+            ve.tensor_reduce(T.land[:, col(j, 1):col(j, 1) + 1], pd[j][:, 0:128], AxisListType.X, A.add,
+                             negate=True).then_inc(sem["vs%d" % p], 1)
+            sa.wait_ge(sem["pm%d" % j], 1)
+            sa.activation(T.jp[:, blk(j)], T.prod[:, blk(j)], ACT.Copy, scale=-1.0,
+                          accum_out=T.land[:, col(j, 3):col(j, 3) + 1]).then_inc(sem["ss%d" % p], 1)
+
+    others = [d for d in T.cores if d != core]
+    mask = topo.mask(core, core)
+    for d in others:
+        mask &= topo.mask(core, d)
+    neng = bin(mask).count("1")
+    ids = []
+    for d in others:
+        rid, pid = topo.addr(d, core)
+        ids.append(DstId(rid=rid, pnc=pid))
+    for p in range(NPH):
+        for j in range(p * NB, p * NB + NB):
+            g.wait_ge(sem["ex%d" % j], 1)
+        g.wait_ge(sem["ss%d" % p], 2 * NB)
+        g.wait_ge(sem["vs%d" % p], NB)
+        o = p * N * W + rank * W
+        g.remote_dma_fused([RemoteDMATransfer(dst_ids=ids, dma_engine_mask=mask, remote_sem=sem["arr%d" % p],
+                                              srcs=[T.land[:, o:o + W]], dsts=[T.land[:, o:o + W] for _ in others],
+                                              alu_op=0)], local_sem=sem.sent)
+
+    nvc = [0]
+    nsc = [0]
+    free = [0]
+
+    def tmp(n):
+        a = free[0]
+        free[0] += (n + 3) // 4 * 4
+        return a
+
+    def cf(a, lo, hi):
+        return T.cf[:, a + lo:a + hi]
+
+    def vstep(ins):
+        ins.then_inc(sem.vc, 1)
+        nvc[0] += 1
+        ve.wait_ge(sem.vc, nvc[0])
+
+    for p in range(NPH):
+        js = range(p * NB, p * NB + NB)
+        base = p * N * W
+        ve.wait_ge(sem["arr%d" % p], neng * len(others))
+        ve.wait_ge(sem["ss%d" % p], 2 * NB)
+        ve.wait_ge(sem["vs%d" % p], NB)
+        t1, t2, S, M = tmp(4 * W), tmp(2 * W), tmp(W), tmp(W)
+        vstep(ve.tensor_tensor(cf(t1, 0, 4 * W), T.land[:, base:base + 4 * W], T.land[:, base + 4 * W:base + 8 * W], A.add))
+        vstep(ve.tensor_tensor(cf(t2, 0, 2 * W), cf(t1, 0, 2 * W), cf(t1, 2 * W, 4 * W), A.add))
+        vstep(ve.tensor_tensor(cf(S, 0, W), cf(t2, 0, W), cf(t2, W, 2 * W), A.add))
+        vstep(ve.tensor_scalar(cf(M, 0, W), cf(S, 0, W), 1.0 / D, None, A.mult))
+        mu, an, m2, m4n = (cf(M, k * NB, (k + 1) * NB) for k in range(4))
+        oP, oV, oVe, oq, oWp, oCn, oEn, ogg, oF = (tmp(NB) for _ in range(9))
+        P, V, Ve, q, Wp, Cn, En, gg, F = (cf(k, 0, NB) for k in (oP, oV, oVe, oq, oWp, oCn, oEn, ogg, oF))
+        vstep(ve.tensor_tensor(P, mu, mu, A.mult))
+        ve.tensor_tensor(V, m2, P, A.subtract).then_inc(sem["vv%d" % p], 1)
+        ve.wait_ge(sem["vv%d" % p], 1)
+        vstep(ve.tensor_scalar(Ve, V, EPS, None, A.add))
+        ve.reciprocal(q, Ve).then_inc(sem["vq%d" % p], 1)
+        ve.wait_ge(sem["vq%d" % p], 1)
+        vstep(ve.tensor_tensor(Wp, mu, an, A.mult))
+        vstep(ve.tensor_tensor(Cn, m4n, Wp, A.subtract))
+        vstep(ve.tensor_tensor(En, Cn, q, A.mult))
+        vstep(ve.tensor_tensor(gg, En, mu, A.mult))
+        vstep(ve.tensor_tensor(F, an, gg, A.subtract))
+        for j in js:
+            jj = j - p * NB
+            vstep(ve.tensor_scalar(T.u[:, blk(j)], T.xT[:, blk(j)], cf(oEn, jj, jj + 1), cf(oF, jj, jj + 1), A.mult, A.add))
+            ve.tensor_tensor(T.inn[:, blk(j)], T.u[:, blk(j)], pd[j][:, 0:128], A.add).then_inc(sem["iv%d" % j], 1)
+
+        osd, ors = p * NB, 8 + p * NB
+        if p == 0:
+            sa.wait_ge(sem.c_id, 1)
+        sa.wait_ge(sem["vv%d" % p], 1)
+        sa.activation(T.cs[:, osd:osd + NB], V, ACT.Sqrt, bias=EPS).then_inc(sem.sc, 1)
+        nsc[0] += 1
+        sa.wait_ge(sem["vq%d" % p], 1)
+        for j in js:
+            jj = j - p * NB
+            sa.wait_ge(sem.sc, nsc[0])
+            sa.activation(T.cs[:, ors + jj:ors + jj + 1], cf(oq, jj, jj + 1), ACT.Copy,
+                          scale=T.cs[:, osd + jj:osd + jj + 1]).then_inc(sem.sc, 1)
+            nsc[0] += 1
+            sa.wait_ge(sem.sc, nsc[0])
+            sa.activation(T.diag[:, blk(j)], T.ident[:], ACT.Copy,
+                          scale=T.cs[:, ors + jj:ors + jj + 1]).then_inc(sem["dg%d" % j], 1)
+
+        te.wait_ge(sem["ss%d" % p], 2 * NB)
+        for j in js:
+            te.wait_ge(sem["ex%d" % j], 1)
+            te.wait_ge(sem["iv%d" % j], 1)
+            te.wait_ge(sem["dg%d" % j], 1)
+            te.matmul(px[j][:, 0:128], T.inn[:, blk(j)], T.diag[:, blk(j)], True, True).then_inc(sem["bk%d" % j], 1)
+
+    for j in range(NBLK):
+        sa.wait_ge(sem["bk%d" % j], 1)
+        sa.activation(T.outb[:, blk(j)], px[j][:, 0:128], ACT.Copy).then_inc(sem["ev%d" % (j // 2)], 1)
+    for h in range(2):
+        c = slice(256 * h, 256 * h + 256)
+        sy.wait_ge(sem["ev%d" % h], 2)
+        sy.dma_start(T.dx[:, c], T.outb[:, c]).then_inc(sem["st%d" % h], 16)
+    for h in range(2):
+        sy.wait_ge(sem["st%d" % h], 16)
+    g.wait_ge(sem.sent, neng * NPH)

@@ -5,10 +5,8 @@ N = 8
 TK = 512
 D = 128 * N
 EPS = 0.01
-NBLK = 4
-NPH = 1
-NB = NBLK // NPH
-W = 4 * NB
+NB = 4
+W = 5 * NB
 
 SCRATCH = {
     "xs": ("sbuf", [128, TK], "float32"),
@@ -17,27 +15,28 @@ SCRATCH = {
     "ident": ("sbuf", [128, 128], "float32"),
     "xT": ("sbuf", [128, TK], "float32"),
     "jq": ("sbuf", [128, TK], "float32"),
+    "jm": ("sbuf", [128, TK], "float32"),
     "prod": ("sbuf", [128, TK], "float32"),
     "jp": ("sbuf", [128, TK], "float32"),
-    "land": ("sbuf", [128, N * 16], "float32"),
-    "cf": ("sbuf", [128, 16 * 16], "float32"),
-    "cs": ("sbuf", [128, 16], "float32"),
+    "land": ("sbuf", [128, N * W], "float32"),
+    "cf": ("sbuf", [128, 256], "float32"),
+    "cs": ("sbuf", [128, 4], "float32"),
+    "dqb": ("sbuf", [128, TK], "float32"),
     "u": ("sbuf", [128, TK], "float32"),
     "inn": ("sbuf", [128, TK], "float32"),
     "diag": ("sbuf", [128, TK], "float32"),
     "outb": ("sbuf", [128, TK], "float32"),
 }
-for _j in range(NBLK):
+for _j in range(NB):
     SCRATCH["px%d" % _j] = ("psum", [128, 512], "float32")
     SCRATCH["pd%d" % _j] = ("psum", [128, 512], "float32")
 
-SEMAPHORES = ["c_ones", "c_id", "vc", "sc", "sent"]
+SEMAPHORES = ["c_ones", "c_id", "sent", "arr", "ss", "sqs", "vs", "epsd", "vv", "vq", "sc"]
+SEMAPHORES += ["v%d" % _k for _k in range(11)]
 for _h in range(2):
     SEMAPHORES += ["ldx%d" % _h, "ldd%d" % _h, "ev%d" % _h, "st%d" % _h]
-for _j in range(NBLK):
-    SEMAPHORES += [_s + str(_j) for _s in ("tx", "td", "ex", "pm", "iv", "dg", "bk")]
-for _p in range(NPH):
-    SEMAPHORES += [_s + str(_p) for _s in ("ss", "vs", "arr", "vv", "vq")]
+for _j in range(NB):
+    SEMAPHORES += [_s + str(_j) for _s in ("tx", "td", "ex", "pm", "dq", "uu", "iv", "dg", "bk")]
 
 
 def rank_program(g, core, T, topo):
@@ -51,12 +50,12 @@ def rank_program(g, core, T, topo):
     def blk(j):
         return slice(128 * j, 128 * j + 128)
 
-    def col(j, s):
-        p, jj = divmod(j, NB)
-        return p * N * W + rank * W + s * NB + jj
+    def own(j, s):
+        c = rank * W + s * NB + j
+        return T.land[:, c:c + 1]
 
-    px = [T["px%d" % j] for j in range(NBLK)]
-    pd = [T["pd%d" % j] for j in range(NBLK)]
+    px = [T["px%d" % j] for j in range(NB)]
+    pd = [T["pd%d" % j] for j in range(NB)]
 
     for h in range(2):
         c = slice(256 * h, 256 * h + 256)
@@ -77,22 +76,21 @@ def rank_program(g, core, T, topo):
         for j in js:
             te.transpose(pd[j][:, 0:128], T.dys[:, blk(j)], T.ident[:]).then_inc(sem["td%d" % j], 1)
         for j in js:
-            p = j // NB
             sa.wait_ge(sem["tx%d" % j], 1)
-            sa.activation(T.xT[:, blk(j)], px[j][:, 0:128], ACT.Copy,
-                          accum_out=T.land[:, col(j, 0):col(j, 0) + 1]).then_inc(sem["ex%d" % j], 1)
-            sa.activation(T.jq[:, blk(j)], px[j][:, 0:128], ACT.Square,
-                          accum_out=T.land[:, col(j, 2):col(j, 2) + 1]).then_inc(sem["ss%d" % p], 1)
+            sa.activation(T.xT[:, blk(j)], px[j][:, 0:128], ACT.Copy, accum_out=own(j, 1)).then_inc(sem["ex%d" % j], 1)
+            sa.activation(T.jq[:, blk(j)], px[j][:, 0:128], ACT.Square, accum_out=own(j, 3)).then_inc(sem.sqs, 1)
+            sa.activation(T.jm[:, blk(j)], px[j][:, 0:128], ACT.Copy, scale=1.0 / D, accum_out=own(j, 0)).then_inc(sem.ss, 1)
+        if h == 1:
+            c = rank * W + 3 * NB
+            ve.wait_ge(sem.sqs, NB)
+            ve.tensor_scalar(T.land[:, c:c + NB], T.land[:, c:c + NB], D * EPS / N, None, A.add).then_inc(sem.epsd, 1)
         for j in js:
-            p = j // NB
             ve.wait_ge(sem["td%d" % j], 1)
             ve.wait_ge(sem["ex%d" % j], 1)
             ve.tensor_tensor(T.prod[:, blk(j)], T.xT[:, blk(j)], pd[j][:, 0:128], A.mult).then_inc(sem["pm%d" % j], 1)
-            ve.tensor_reduce(T.land[:, col(j, 1):col(j, 1) + 1], pd[j][:, 0:128], AxisListType.X, A.add,
-                             negate=True).then_inc(sem["vs%d" % p], 1)
+            ve.tensor_reduce(own(j, 2), pd[j][:, 0:128], AxisListType.X, A.add, negate=True).then_inc(sem.vs, 1)
             sa.wait_ge(sem["pm%d" % j], 1)
-            sa.activation(T.jp[:, blk(j)], T.prod[:, blk(j)], ACT.Copy, scale=-1.0,
-                          accum_out=T.land[:, col(j, 3):col(j, 3) + 1]).then_inc(sem["ss%d" % p], 1)
+            sa.activation(T.jp[:, blk(j)], T.prod[:, blk(j)], ACT.Copy, scale=-1.0, accum_out=own(j, 4)).then_inc(sem.ss, 1)
 
     others = [d for d in T.cores if d != core]
     mask = topo.mask(core, core)
@@ -103,18 +101,16 @@ def rank_program(g, core, T, topo):
     for d in others:
         rid, pid = topo.addr(d, core)
         ids.append(DstId(rid=rid, pnc=pid))
-    for p in range(NPH):
-        for j in range(p * NB, p * NB + NB):
-            g.wait_ge(sem["ex%d" % j], 1)
-        g.wait_ge(sem["ss%d" % p], 2 * NB)
-        g.wait_ge(sem["vs%d" % p], NB)
-        o = p * N * W + rank * W
-        g.remote_dma_fused([RemoteDMATransfer(dst_ids=ids, dma_engine_mask=mask, remote_sem=sem["arr%d" % p],
-                                              srcs=[T.land[:, o:o + W]], dsts=[T.land[:, o:o + W] for _ in others],
-                                              alu_op=0)], local_sem=sem.sent)
+    for j in range(NB):
+        g.wait_ge(sem["ex%d" % j], 1)
+    g.wait_ge(sem.epsd, 1)
+    g.wait_ge(sem.vs, NB)
+    g.wait_ge(sem.ss, 2 * NB)
+    o = rank * W
+    g.remote_dma_fused([RemoteDMATransfer(dst_ids=ids, dma_engine_mask=mask, remote_sem=sem.arr,
+                                          srcs=[T.land[:, o:o + W]], dsts=[T.land[:, o:o + W] for _ in others],
+                                          alu_op=0)], local_sem=sem.sent)
 
-    nvc = [0]
-    nsc = [0]
     free = [0]
 
     def tmp(n):
@@ -125,66 +121,72 @@ def rank_program(g, core, T, topo):
     def cf(a, lo, hi):
         return T.cf[:, a + lo:a + hi]
 
-    def vstep(ins):
-        ins.then_inc(sem.vc, 1)
-        nvc[0] += 1
-        ve.wait_ge(sem.vc, nvc[0])
+    ve.wait_ge(sem.epsd, 1)
+    ve.wait_ge(sem.vs, NB)
+    ve.wait_ge(sem.ss, 2 * NB)
+    ve.wait_ge(sem.arr, neng * len(others))
+    t1, t2, S = tmp(4 * W), tmp(2 * W), tmp(W)
+    ve.tensor_tensor(cf(t1, 0, 4 * W), T.land[:, 0:4 * W], T.land[:, 4 * W:8 * W], A.add).then_inc(sem.v0, 1)
+    ve.wait_ge(sem.v0, 1)
+    ve.tensor_tensor(cf(t2, 0, 2 * W), cf(t1, 0, 2 * W), cf(t1, 2 * W, 4 * W), A.add).then_inc(sem.v1, 1)
+    ve.wait_ge(sem.v1, 1)
+    ve.tensor_tensor(cf(S, 0, W), cf(t2, 0, W), cf(t2, W, 2 * W), A.add).then_inc(sem.v2, 1)
+    ve.wait_ge(sem.v2, 1)
+    mu, s1, s3n, s2e, s4n = (cf(S, k * NB, (k + 1) * NB) for k in range(5))
+    oP, oWr, ovr, oCr, oq, oan, oCm, oEn, ogg, oF = (tmp(NB) for _ in range(10))
+    P, Wr, vr, Cr, q, an, Cm, En, gg, F = (cf(k, 0, NB) for k in (oP, oWr, ovr, oCr, oq, oan, oCm, oEn, ogg, oF))
+    ve.tensor_tensor(P, mu, s1, A.mult).then_inc(sem.v3, 1)
+    ve.tensor_tensor(Wr, mu, s3n, A.mult).then_inc(sem.v4, 1)
+    ve.wait_ge(sem.v3, 1)
+    ve.tensor_tensor(vr, s2e, P, A.subtract).then_inc(sem.vv, 1)
+    ve.wait_ge(sem.v4, 1)
+    ve.tensor_tensor(Cr, s4n, Wr, A.subtract).then_inc(sem.v5, 1)
+    ve.wait_ge(sem.vv, 1)
+    ve.reciprocal(q, vr).then_inc(sem.vq, 1)
+    ve.tensor_scalar(an, s3n, 1.0 / D, None, A.mult).then_inc(sem.v6, 1)
+    ve.wait_ge(sem.v5, 1)
+    ve.tensor_tensor(Cm, Cr, mu, A.mult).then_inc(sem.v7, 1)
+    ve.wait_ge(sem.vq, 1)
+    ve.tensor_tensor(En, Cr, q, A.mult).then_inc(sem.v8, 1)
+    ve.wait_ge(sem.v7, 1)
+    ve.tensor_tensor(gg, Cm, q, A.mult).then_inc(sem.v9, 1)
 
-    for p in range(NPH):
-        js = range(p * NB, p * NB + NB)
-        base = p * N * W
-        ve.wait_ge(sem["arr%d" % p], neng * len(others))
-        ve.wait_ge(sem["ss%d" % p], 2 * NB)
-        ve.wait_ge(sem["vs%d" % p], NB)
-        t1, t2, S, M = tmp(4 * W), tmp(2 * W), tmp(W), tmp(W)
-        vstep(ve.tensor_tensor(cf(t1, 0, 4 * W), T.land[:, base:base + 4 * W], T.land[:, base + 4 * W:base + 8 * W], A.add))
-        vstep(ve.tensor_tensor(cf(t2, 0, 2 * W), cf(t1, 0, 2 * W), cf(t1, 2 * W, 4 * W), A.add))
-        vstep(ve.tensor_tensor(cf(S, 0, W), cf(t2, 0, W), cf(t2, W, 2 * W), A.add))
-        vstep(ve.tensor_scalar(cf(M, 0, W), cf(S, 0, W), 1.0 / D, None, A.mult))
-        mu, an, m2, m4n = (cf(M, k * NB, (k + 1) * NB) for k in range(4))
-        oP, oV, oVe, oq, oWp, oCn, oEn, ogg, oF = (tmp(NB) for _ in range(9))
-        P, V, Ve, q, Wp, Cn, En, gg, F = (cf(k, 0, NB) for k in (oP, oV, oVe, oq, oWp, oCn, oEn, ogg, oF))
-        vstep(ve.tensor_tensor(P, mu, mu, A.mult))
-        ve.tensor_tensor(V, m2, P, A.subtract).then_inc(sem["vv%d" % p], 1)
-        ve.wait_ge(sem["vv%d" % p], 1)
-        vstep(ve.tensor_scalar(Ve, V, EPS, None, A.add))
-        ve.reciprocal(q, Ve).then_inc(sem["vq%d" % p], 1)
-        ve.wait_ge(sem["vq%d" % p], 1)
-        vstep(ve.tensor_tensor(Wp, mu, an, A.mult))
-        vstep(ve.tensor_tensor(Cn, m4n, Wp, A.subtract))
-        vstep(ve.tensor_tensor(En, Cn, q, A.mult))
-        vstep(ve.tensor_tensor(gg, En, mu, A.mult))
-        vstep(ve.tensor_tensor(F, an, gg, A.subtract))
-        for j in js:
-            jj = j - p * NB
-            vstep(ve.tensor_scalar(T.u[:, blk(j)], T.xT[:, blk(j)], cf(oEn, jj, jj + 1), cf(oF, jj, jj + 1), A.mult, A.add))
-            ve.tensor_tensor(T.inn[:, blk(j)], T.u[:, blk(j)], pd[j][:, 0:128], A.add).then_inc(sem["iv%d" % j], 1)
+    def dq(j):
+        ve.tensor_scalar(T.dqb[:, blk(j)], T.ident[:], cf(oq, j, j + 1), float(D), A.mult, A.mult).then_inc(sem["dq%d" % j], 1)
 
-        osd, ors = p * NB, 8 + p * NB
-        if p == 0:
-            sa.wait_ge(sem.c_id, 1)
-        sa.wait_ge(sem["vv%d" % p], 1)
-        sa.activation(T.cs[:, osd:osd + NB], V, ACT.Sqrt, bias=EPS).then_inc(sem.sc, 1)
-        nsc[0] += 1
-        sa.wait_ge(sem["vq%d" % p], 1)
-        for j in js:
-            jj = j - p * NB
-            sa.wait_ge(sem.sc, nsc[0])
-            sa.activation(T.cs[:, ors + jj:ors + jj + 1], cf(oq, jj, jj + 1), ACT.Copy,
-                          scale=T.cs[:, osd + jj:osd + jj + 1]).then_inc(sem.sc, 1)
-            nsc[0] += 1
-            sa.wait_ge(sem.sc, nsc[0])
-            sa.activation(T.diag[:, blk(j)], T.ident[:], ACT.Copy,
-                          scale=T.cs[:, ors + jj:ors + jj + 1]).then_inc(sem["dg%d" % j], 1)
+    ve.wait_ge(sem.c_id, 1)
+    dq(0)
+    dq(1)
+    ve.wait_ge(sem.v6, 1)
+    ve.wait_ge(sem.v9, 1)
+    ve.tensor_tensor(F, an, gg, A.subtract).then_inc(sem.v10, 1)
+    dq(2)
+    dq(3)
+    ve.wait_ge(sem.v8, 1)
+    ve.wait_ge(sem.v10, 1)
+    for j in range(NB):
+        ve.tensor_scalar(T.u[:, blk(j)], T.xT[:, blk(j)], cf(oEn, j, j + 1), cf(oF, j, j + 1),
+                         A.mult, A.add).then_inc(sem["uu%d" % j], 1)
+    for j in range(NB):
+        ve.wait_ge(sem["uu%d" % j], 1)
+        ve.tensor_tensor(T.inn[:, blk(j)], T.u[:, blk(j)], pd[j][:, 0:128], A.add).then_inc(sem["iv%d" % j], 1)
 
-        te.wait_ge(sem["ss%d" % p], 2 * NB)
-        for j in js:
-            te.wait_ge(sem["ex%d" % j], 1)
-            te.wait_ge(sem["iv%d" % j], 1)
-            te.wait_ge(sem["dg%d" % j], 1)
-            te.matmul(px[j][:, 0:128], T.inn[:, blk(j)], T.diag[:, blk(j)], True, True).then_inc(sem["bk%d" % j], 1)
+    sa.wait_ge(sem.vv, 1)
+    sa.activation(T.cs[:, 0:NB], vr, ACT.Sqrt, scale=1.0 / D).then_inc(sem.sc, 1)
+    sa.wait_ge(sem.sc, 1)
+    for j in range(NB):
+        sa.wait_ge(sem["dq%d" % j], 1)
+        sa.activation(T.diag[:, blk(j)], T.dqb[:, blk(j)], ACT.Copy, scale=T.cs[:, j:j + 1]).then_inc(sem["dg%d" % j], 1)
 
-    for j in range(NBLK):
+    te.wait_ge(sem.sqs, NB)
+    te.wait_ge(sem.ss, 2 * NB)
+    for j in range(NB):
+        te.wait_ge(sem["ex%d" % j], 1)
+        te.wait_ge(sem["iv%d" % j], 1)
+        te.wait_ge(sem["dg%d" % j], 1)
+        te.matmul(px[j][:, 0:128], T.inn[:, blk(j)], T.diag[:, blk(j)], True, True).then_inc(sem["bk%d" % j], 1)
+
+    for j in range(NB):
         sa.wait_ge(sem["bk%d" % j], 1)
         sa.activation(T.outb[:, blk(j)], px[j][:, 0:128], ACT.Copy).then_inc(sem["ev%d" % (j // 2)], 1)
     for h in range(2):
@@ -193,4 +195,4 @@ def rank_program(g, core, T, topo):
         sy.dma_start(T.dx[:, c], T.outb[:, c]).then_inc(sem["st%d" % h], 16)
     for h in range(2):
         sy.wait_ge(sem["st%d" % h], 16)
-    g.wait_ge(sem.sent, neng * NPH)
+    g.wait_ge(sem.sent, neng)

from concourse.bass import DstId, RemoteDMATransfer
from concourse.mybir import AluOpType, AxisListType, ActivationFunctionType

N = 8
TK = 512
D = 128 * N
EPS = 0.01
NB = 4
W = 5 * NB

SCRATCH = {
    "xs": ("sbuf", [128, TK], "float32"),
    "dys": ("sbuf", [128, TK], "float32"),
    "ones": ("sbuf", [128, 128], "float32"),
    "ident": ("sbuf", [128, 128], "float32"),
    "xT": ("sbuf", [128, TK], "float32"),
    "jq": ("sbuf", [128, TK], "float32"),
    "jm": ("sbuf", [128, TK], "float32"),
    "prod": ("sbuf", [128, TK], "float32"),
    "jp": ("sbuf", [128, TK], "float32"),
    "land": ("sbuf", [128, N * W], "float32"),
    "cf": ("sbuf", [128, 256], "float32"),
    "cs": ("sbuf", [128, 4], "float32"),
    "dqb": ("sbuf", [128, TK], "float32"),
    "u": ("sbuf", [128, TK], "float32"),
    "inn": ("sbuf", [128, TK], "float32"),
    "diag": ("sbuf", [128, TK], "float32"),
    "outb": ("sbuf", [128, TK], "float32"),
}
for _j in range(NB):
    SCRATCH["px%d" % _j] = ("psum", [128, 512], "float32")
    SCRATCH["pd%d" % _j] = ("psum", [128, 512], "float32")

SEMAPHORES = ["c_ones", "c_id", "sent", "arr", "ss", "sqs", "vs", "epsd", "vv", "vq", "sc"]
SEMAPHORES += ["v%d" % _k for _k in range(11)]
for _h in range(2):
    SEMAPHORES += ["ldx%d" % _h, "ldd%d" % _h, "ev%d" % _h, "st%d" % _h]
for _j in range(NB):
    SEMAPHORES += [_s + str(_j) for _s in ("tx", "td", "ex", "pm", "dq", "uu", "iv", "dg", "bk")]


def rank_program(g, core, T, topo):
    rank = T.rank_of(core)
    if rank is None:
        return
    sem = T.sem
    A, ACT = AluOpType, ActivationFunctionType
    te, ve, sa, sy = g.tensor, g.vector, g.scalar, g.sync

    def blk(j):
        return slice(128 * j, 128 * j + 128)

    def own(j, s):
        c = rank * W + s * NB + j
        return T.land[:, c:c + 1]

    px = [T["px%d" % j] for j in range(NB)]
    pd = [T["pd%d" % j] for j in range(NB)]

    for h in range(2):
        c = slice(256 * h, 256 * h + 256)
        sy.dma_start(T.xs[:, c], T.x[:, c]).then_inc(sem["ldx%d" % h], 16)
        sy.dma_start(T.dys[:, c], T.dy[:, c]).then_inc(sem["ldd%d" % h], 16)

    ve.memset(T.ones[:], 1.0).then_inc(sem.c_ones, 1)
    g.wait_ge(sem.c_ones, 1)
    g.affine_select(T.ident[:], T.ones[:], [[-1, 128]], A.is_equal, 0.0, 0, 1).then_inc(sem.c_id, 1)

    te.wait_ge(sem.c_id, 1)
    for h in range(2):
        js = (2 * h, 2 * h + 1)
        te.wait_ge(sem["ldx%d" % h], 16)
        for j in js:
            te.transpose(px[j][:, 0:128], T.xs[:, blk(j)], T.ident[:]).then_inc(sem["tx%d" % j], 1)
        te.wait_ge(sem["ldd%d" % h], 16)
        for j in js:
            te.transpose(pd[j][:, 0:128], T.dys[:, blk(j)], T.ident[:]).then_inc(sem["td%d" % j], 1)
        for j in js:
            sa.wait_ge(sem["tx%d" % j], 1)
            sa.activation(T.xT[:, blk(j)], px[j][:, 0:128], ACT.Copy, accum_out=own(j, 1)).then_inc(sem["ex%d" % j], 1)
            sa.activation(T.jq[:, blk(j)], px[j][:, 0:128], ACT.Square, accum_out=own(j, 3)).then_inc(sem.sqs, 1)
            sa.activation(T.jm[:, blk(j)], px[j][:, 0:128], ACT.Copy, scale=1.0 / D, accum_out=own(j, 0)).then_inc(sem.ss, 1)
        if h == 1:
            c = rank * W + 3 * NB
            ve.wait_ge(sem.sqs, NB)
            ve.tensor_scalar(T.land[:, c:c + NB], T.land[:, c:c + NB], D * EPS / N, None, A.add).then_inc(sem.epsd, 1)
        for j in js:
            ve.wait_ge(sem["td%d" % j], 1)
            ve.wait_ge(sem["ex%d" % j], 1)
            ve.tensor_tensor(T.prod[:, blk(j)], T.xT[:, blk(j)], pd[j][:, 0:128], A.mult).then_inc(sem["pm%d" % j], 1)
            ve.tensor_reduce(own(j, 2), pd[j][:, 0:128], AxisListType.X, A.add, negate=True).then_inc(sem.vs, 1)
            sa.wait_ge(sem["pm%d" % j], 1)
            sa.activation(T.jp[:, blk(j)], T.prod[:, blk(j)], ACT.Copy, scale=-1.0, accum_out=own(j, 4)).then_inc(sem.ss, 1)

    others = [d for d in T.cores if d != core]
    mask = topo.mask(core, core)
    for d in others:
        mask &= topo.mask(core, d)
    neng = bin(mask).count("1")
    ids = []
    for d in others:
        rid, pid = topo.addr(d, core)
        ids.append(DstId(rid=rid, pnc=pid))
    for j in range(NB):
        g.wait_ge(sem["ex%d" % j], 1)
    g.wait_ge(sem.epsd, 1)
    g.wait_ge(sem.vs, NB)
    g.wait_ge(sem.ss, 2 * NB)
    o = rank * W
    g.remote_dma_fused([RemoteDMATransfer(dst_ids=ids, dma_engine_mask=mask, remote_sem=sem.arr,
                                          srcs=[T.land[:, o:o + W]], dsts=[T.land[:, o:o + W] for _ in others],
                                          alu_op=0)], local_sem=sem.sent)

    free = [0]

    def tmp(n):
        a = free[0]
        free[0] += (n + 3) // 4 * 4
        return a

    def cf(a, lo, hi):
        return T.cf[:, a + lo:a + hi]

    ve.wait_ge(sem.epsd, 1)
    ve.wait_ge(sem.vs, NB)
    ve.wait_ge(sem.ss, 2 * NB)
    ve.wait_ge(sem.arr, neng * len(others))
    t1, t2, S = tmp(4 * W), tmp(2 * W), tmp(W)
    ve.tensor_tensor(cf(t1, 0, 4 * W), T.land[:, 0:4 * W], T.land[:, 4 * W:8 * W], A.add).then_inc(sem.v0, 1)
    ve.wait_ge(sem.v0, 1)
    ve.tensor_tensor(cf(t2, 0, 2 * W), cf(t1, 0, 2 * W), cf(t1, 2 * W, 4 * W), A.add).then_inc(sem.v1, 1)
    ve.wait_ge(sem.v1, 1)
    ve.tensor_tensor(cf(S, 0, W), cf(t2, 0, W), cf(t2, W, 2 * W), A.add).then_inc(sem.v2, 1)
    ve.wait_ge(sem.v2, 1)
    mu, s1, s3n, s2e, s4n = (cf(S, k * NB, (k + 1) * NB) for k in range(5))
    oP, oWr, ovr, oCr, oq, oan, oCm, oEn, ogg, oF = (tmp(NB) for _ in range(10))
    P, Wr, vr, Cr, q, an, Cm, En, gg, F = (cf(k, 0, NB) for k in (oP, oWr, ovr, oCr, oq, oan, oCm, oEn, ogg, oF))
    ve.tensor_tensor(P, mu, s1, A.mult).then_inc(sem.v3, 1)
    ve.tensor_tensor(Wr, mu, s3n, A.mult).then_inc(sem.v4, 1)
    ve.wait_ge(sem.v3, 1)
    ve.tensor_tensor(vr, s2e, P, A.subtract).then_inc(sem.vv, 1)
    ve.wait_ge(sem.v4, 1)
    ve.tensor_tensor(Cr, s4n, Wr, A.subtract).then_inc(sem.v5, 1)
    ve.wait_ge(sem.vv, 1)
    ve.reciprocal(q, vr).then_inc(sem.vq, 1)
    ve.tensor_scalar(an, s3n, 1.0 / D, None, A.mult).then_inc(sem.v6, 1)
    ve.wait_ge(sem.v5, 1)
    ve.tensor_tensor(Cm, Cr, mu, A.mult).then_inc(sem.v7, 1)
    ve.wait_ge(sem.vq, 1)
    ve.tensor_tensor(En, Cr, q, A.mult).then_inc(sem.v8, 1)
    ve.wait_ge(sem.v7, 1)
    ve.tensor_tensor(gg, Cm, q, A.mult).then_inc(sem.v9, 1)

    def dq(j):
        ve.tensor_scalar(T.dqb[:, blk(j)], T.ident[:], cf(oq, j, j + 1), float(D), A.mult, A.mult).then_inc(sem["dq%d" % j], 1)

    ve.wait_ge(sem.c_id, 1)
    dq(0)
    dq(1)
    ve.wait_ge(sem.v6, 1)
    ve.wait_ge(sem.v9, 1)
    ve.tensor_tensor(F, an, gg, A.subtract).then_inc(sem.v10, 1)
    dq(2)
    dq(3)
    ve.wait_ge(sem.v8, 1)
    ve.wait_ge(sem.v10, 1)
    for j in range(NB):
        ve.tensor_scalar(T.u[:, blk(j)], T.xT[:, blk(j)], cf(oEn, j, j + 1), cf(oF, j, j + 1),
                         A.mult, A.add).then_inc(sem["uu%d" % j], 1)
    for j in range(NB):
        ve.wait_ge(sem["uu%d" % j], 1)
        ve.tensor_tensor(T.inn[:, blk(j)], T.u[:, blk(j)], pd[j][:, 0:128], A.add).then_inc(sem["iv%d" % j], 1)

    sa.wait_ge(sem.vv, 1)
    sa.activation(T.cs[:, 0:NB], vr, ACT.Sqrt, scale=1.0 / D).then_inc(sem.sc, 1)
    sa.wait_ge(sem.sc, 1)
    for j in range(NB):
        sa.wait_ge(sem["dq%d" % j], 1)
        sa.activation(T.diag[:, blk(j)], T.dqb[:, blk(j)], ACT.Copy, scale=T.cs[:, j:j + 1]).then_inc(sem["dg%d" % j], 1)

    te.wait_ge(sem.sqs, NB)
    te.wait_ge(sem.ss, 2 * NB)
    for j in range(NB):
        te.wait_ge(sem["ex%d" % j], 1)
        te.wait_ge(sem["iv%d" % j], 1)
        te.wait_ge(sem["dg%d" % j], 1)
        te.matmul(px[j][:, 0:128], T.inn[:, blk(j)], T.diag[:, blk(j)], True, True).then_inc(sem["bk%d" % j], 1)

    for j in range(NB):
        sa.wait_ge(sem["bk%d" % j], 1)
        sa.activation(T.outb[:, blk(j)], px[j][:, 0:128], ACT.Copy).then_inc(sem["ev%d" % (j // 2)], 1)
    for h in range(2):
        c = slice(256 * h, 256 * h + 256)
        sy.wait_ge(sem["ev%d" % h], 2)
        sy.dma_start(T.dx[:, c], T.outb[:, c]).then_inc(sem["st%d" % h], 16)
    for h in range(2):
        sy.wait_ge(sem["st%d" % h], 16)
    g.wait_ge(sem.sent, neng)
